import numpy as np
import ml_dtypes


def mxq(x, axis, fmt="e4m3"):
    dtype, down = {"e4m3": (ml_dtypes.float8_e4m3fn, 7), "e5m2": (ml_dtypes.float8_e5m2, 14)}[fmt]
    v = np.moveaxis(np.asarray(x, np.float32).astype(ml_dtypes.bfloat16).astype(np.float64), axis, -1)
    blocks = v.reshape(v.shape[:-1] + (-1, 32))
    amax = np.abs(blocks).max(-1, keepdims=True)
    byte = np.maximum(np.where(amax > 0, np.frexp(amax)[1] - 1 + 127, 0) - down, 1)
    scale = np.exp2(byte - 127.0)
    codes = (blocks / scale).astype(np.float32).astype(dtype).astype(np.float64)
    return np.moveaxis((codes * scale).reshape(v.shape), -1, axis)


WIDE = False


def mx_kscale(k):
    if not WIDE:
        return np.ones(k)
    levels = np.array([10, -10, 5, -5, 0])
    if k % 512:
        return np.exp2(np.random.permutation(np.resize(levels, k // 32))).repeat(32)
    a = np.empty((k // 512, 16))
    for p in range(k // 512):
        a[p, :8] = np.random.permutation(np.resize(levels, 8))
        for g in range(8):
            far = levels[np.abs(levels - a[p, g]) >= 10]
            a[p, g + 8] = far[np.random.randint(len(far))]
    return np.exp2(a.ravel()).repeat(32)


BF16 = ml_dtypes.bfloat16


def bf(x):
    return np.asarray(x, np.float32).astype(BF16)


def f64(x):
    return np.asarray(x).astype(np.float64)


E2M1 = np.array([0.0, 0.5, 1.0, 1.5, 2.0, 3.0, 4.0, 6.0, -0.0, -0.5, -1.0, -1.5, -2.0, -3.0, -4.0, -6.0])


def pack_weight(w, fmt):
    k, n = w.shape
    w = f64(bf(w)).reshape(k // 32, 32, n)
    amax = np.abs(w).max(1)
    if fmt == "e4m3":
        byte = np.frexp(amax)[1] - 1 + 127 - 7
    else:
        mant, ex = np.frexp(amax / 6.0)
        byte = np.where(mant > 0.5, ex, ex - 1) + 127
    byte = np.clip(np.where(amax > 0, byte, 1), 1, 254)
    scaled = (w * np.exp2(127.0 - byte)[:, None, :]).reshape(k, n).astype(np.float32)
    by_word = np.ascontiguousarray(scaled.reshape(k // 512, 128, 4, n).transpose(0, 1, 3, 2))
    if fmt == "e4m3":
        words = by_word.astype(ml_dtypes.float8_e4m3fn).view(np.uint8)
    else:
        c = by_word.astype(ml_dtypes.float4_e2m1fn).view(np.uint8) & 0xF
        words = c[..., 0::2] | (c[..., 1::2] << 4)
    return np.ascontiguousarray(words), np.ascontiguousarray(byte.astype(np.uint8).reshape(k // 512, 16, n))


def unpack_weight(words, scales, fmt):
    g, p, n, _ = words.shape
    if fmt == "e4m3":
        vals = np.ascontiguousarray(words).view(ml_dtypes.float8_e4m3fn).astype(np.float64)
    else:
        nib = np.empty((g, p, n, 4), np.uint8)
        nib[..., 0::2] = words & 0xF
        nib[..., 1::2] = words >> 4
        vals = E2M1[nib]
    vals = vals * np.repeat(np.exp2(scales.astype(np.float64) - 127.0), 8, axis=1)[..., None]
    return vals.transpose(0, 1, 3, 2).reshape(g * 512, n)
def pack4(w):
    words, scales = pack_weight(w, "e2m1")
    return words.reshape(words.shape[0], 128, -1), scales


def unpack4(words, scales):
    return unpack_weight(words.reshape(words.shape[0], 128, -1, 2), scales, "e2m1")


M, KH, KT, N = 1024, 1024, 3072, 1024


def setup_inputs():
    s, t = mx_kscale(KH), mx_kscale(KT)
    u_tail = np.random.standard_normal((KT, N)) / np.sqrt(KT) / t[:, None]
    u_tail_words, u_tail_scales = pack4(u_tail)
    return {"tf_head": bf(np.abs(np.random.standard_normal((M, KH)))),
            "tf_tail": bf(np.maximum(np.random.standard_normal((M, KT)), 0.0)),
            "idf_head": bf((0.5 + np.random.random_sample(KH)) * s),
            "idf_tail": bf((1.0 + 2.0 * np.random.random_sample(KT)) * t),
            "u_head": bf(np.random.standard_normal((KH, N)) / np.sqrt(KH) / s[:, None]),
            "u_tail_words": u_tail_words,
            "u_tail_scales": u_tail_scales,
            "sigma": bf(0.5 + 1.5 * np.random.random_sample(N)),
            "docs": bf(np.random.standard_normal((M, N)) / np.sqrt(N))}


def reference(tf_head, tf_tail, idf_head, idf_tail, u_head, u_tail_words, u_tail_scales, sigma, docs):
    x_head = f64(tf_head) * f64(idf_head)
    x_tail = f64(tf_tail) * f64(idf_tail)
    u_tail = unpack4(u_tail_words, u_tail_scales)
    head = mxq(x_head, 1, "e4m3") @ mxq(f64(u_head), 0, "e4m3")
    tail = mxq(x_tail, 1, "e4m3") @ u_tail
    concepts = (head + tail) / f64(sigma)
    scores = np.sum(concepts * f64(docs), axis=1, keepdims=True)
    return concepts, scores

@@ -1,0 +1,356 @@
+from contextlib import ExitStack
+
+import concourse.mybir as mybir
+from concourse.masks import make_identity
+
+M, KH, KT, N = 1024, 1024, 3072, 1024
+FLOPS = 2 * M * (KH + KT) * N
+
+F32 = mybir.dt.float32
+BF16 = mybir.dt.bfloat16
+I32 = mybir.dt.int32
+U32 = mybir.dt.uint32
+U8 = mybir.dt.uint8
+FP8X4 = mybir.dt.float8_e4m3fn_x4
+FP4X4 = mybir.dt.float4_e2m1fn_x4
+MULT = mybir.AluOpType.mult
+ADD = mybir.AluOpType.add
+COPY = mybir.ActivationFunctionType.Copy
+
+P = 128
+K_PASS = 512
+TAIL_PASSES = KT // K_PASS
+HEAD_PASSES = KH // K_PASS
+PASSES = TAIL_PASSES + HEAD_PASSES
+TILES = M // P
+HALF = 512
+PAIRS = PASSES // 2
+TURN_BANKS = 4
+
+
+def tile_lsi_query_fold_in_s1_kernel(
+    tc, tf_head, tf_tail, idf_head, idf_tail, u_head, u_tail_words, u_tail_scales, sigma, docs, out_0, out_1
+):
+    nc = tc.nc
+    tf_tail_v = tf_tail.rearrange("(p m) k -> p m k", m=TILES)
+    tf_head_v = tf_head.rearrange("(p m) k -> p m k", m=TILES)
+    docs_v = docs.rearrange("(p m) n -> p m n", m=TILES)
+    concepts_v = out_0.rearrange("(p m) n -> p m n", m=TILES)
+    scores_v = out_1.rearrange("(p m) o -> p (m o)", m=TILES)
+
+    with ExitStack() as ctx:
+        keep = ctx.enter_context(tc.tile_pool(name="keep", bufs=1))
+        work = ctx.enter_context(tc.tile_pool(name="work", bufs=2))
+        psum = ctx.enter_context(tc.psum_pool(name="psum", bufs=1))
+        ctx.enter_context(tc.manual_schedule())
+
+        ident = keep.tile([P, P], F32)
+        rows = keep.tile([P, K_PASS], BF16)
+        idf_tail_words = keep.tile([P, TAIL_PASSES, 2], F32)
+        late_words = keep.tile([P, 4, 2], F32)
+        inv_sigma_col = keep.tile([P, 8], F32)
+        inv_sigma = keep.tile([P, N], F32)
+        ut_scales = keep.tile([P, TAIL_PASSES, N], U8, align_bytes=64)
+        uh_codes = keep.tile([P, HEAD_PASSES, N], U32, align_bytes=64)
+        uh_scales = keep.tile([P, HEAD_PASSES, N], U8, align_bytes=64)
+        scores = keep.tile([P, TILES], F32)
+        last_parts = keep.tile([P, 2], F32)
+
+        tf_words = {}
+        ut_words = {}
+        uh_raw = {}
+        docs_sb = {}
+
+        def load_tf_tail(m, first, count):
+            raw = keep.tile([P, count * K_PASS], BF16, name="tf_tail_%d_%d" % (m, first))
+            nc.sync.dma_start(out=raw[:], in_=tf_tail_v[:, m, first * K_PASS : (first + count) * K_PASS])
+            tf_words[m, first] = raw[:].bitcast(F32)
+            for g in range(first, first + count):
+                tf_words[m, g, "pass"] = raw[:].bitcast(F32)[:, (g - first) * 256 : (g - first + 1) * 256]
+
+        def load_tf_head(m):
+            raw = keep.tile([P, 2 * KH], BF16, name="tf_head_%d" % m)
+            nc.sync.dma_start(out=raw[:], in_=tf_head_v[:, m : m + 2, :].rearrange("p m k -> p (m k)"))
+            for i in range(2):
+                tf_words[m + i, TAIL_PASSES] = raw[:].bitcast(F32)[:, i * 512 : (i + 1) * 512]
+                for g in range(HEAD_PASSES):
+                    tf_words[m + i, TAIL_PASSES + g, "pass"] = raw[:].bitcast(F32)[
+                        :, i * 512 + g * 256 : i * 512 + (g + 1) * 256
+                    ]
+
+        def load_ut_words(pair):
+            raw = keep.tile([P, 2, 2 * N], U8, name="ut_words_%d" % pair, align_bytes=64)
+            nc.sync.dma_start(
+                out=raw[:].bitcast(I32),
+                in_=u_tail_words[2 * pair : 2 * pair + 2].rearrange("g p n -> p g n").bitcast(I32),
+            )
+            ut_words[pair] = raw
+
+        def load_u_head(g):
+            raw = keep.tile([P, 4, N], BF16, name="u_head_%d" % g)
+            nc.sync.dma_start(
+                out=raw[:], in_=u_head[g * K_PASS : (g + 1) * K_PASS, :].rearrange("(p t) n -> p t n", t=4)
+            )
+            uh_raw[g] = raw
+
+        def load_docs(m):
+            raw = keep.tile([P, 2, N], BF16, name="docs_%d" % m)
+            nc.sync.dma_start(out=raw[:], in_=docs_v[:, m : m + 2, :])
+            docs_sb[m] = raw[:, 0, :]
+            docs_sb[m + 1] = raw[:, 1, :]
+
+        turn_count = []
+
+        def next_turn_bank():
+            tag = "turn%d" % (len(turn_count) % TURN_BANKS)
+            turn_count.append(tag)
+            return psum.tile([P, 2, 2, P], F32, name=tag, tag=tag)
+
+        sorted_words = {}
+        turned = {}
+        grouped = {}
+        x_codes = {}
+        x_scales = {}
+        acc = {}
+        concepts = {}
+        products = {}
+
+        def sort_words(m):
+            out = work.tile([P, PASSES, 2, P], F32, name="sorted", tag="sorted")
+            nc.scalar.copy(
+                out=out[:, 0:TAIL_PASSES],
+                in_=tf_words[m, 0].rearrange("p (g w u) -> p g u w", u=2, w=P),
+            )
+            nc.scalar.copy(
+                out=out[:, TAIL_PASSES:PASSES],
+                in_=tf_words[m, TAIL_PASSES].rearrange("p (g w u) -> p g u w", u=2, w=P),
+            )
+            sorted_words[m] = out
+
+        def turn(m, pair):
+            bank = next_turn_bank()
+            for i in range(2):
+                g = 2 * pair + i
+                for u in range(2):
+                    if m in sorted_words:
+                        src = sorted_words[m][:, g, u, :]
+                    else:
+                        src = tf_words[m, g, "pass"][:, u:256:2]
+                    nc.tensor.transpose(bank[:, u, i, :], src, ident[:])
+            turned[m, pair] = bank
+
+        def weigh(m, pair):
+            if m not in grouped:
+                grouped[m] = work.tile([P, PASSES, P, 4], BF16, name="grouped", tag="grouped", align_bytes=64)
+                x_codes[m] = work.tile([P, PASSES, P], U32, name="x_codes", tag="x_codes", bufs=3, align_bytes=64)
+                x_scales[m] = work.tile([P, PASSES, P], U8, name="x_scales", tag="x_scales", bufs=3, align_bytes=64)
+            if pair < PAIRS - 1:
+                idf = idf_tail_words[:, 2 * pair : 2 * pair + 2, :]
+            else:
+                idf = late_words[:, 0:2, :]
+            idf = idf.bitcast(BF16).rearrange("p g (u e) -> p g u e", e=2).unsqueeze(2).broadcast_to([P, 2, P, 2, 2])
+            nc.vector.tensor_tensor(
+                out=grouped[m][:, 2 * pair : 2 * pair + 2].rearrange("p g r (u e) -> p g r u e", e=2),
+                in0=turned[m, pair][:].bitcast(BF16).rearrange("p u g (r e) -> p g r u e", e=2),
+                in1=idf,
+                op=MULT,
+            )
+
+        def quantize_x(m, first, count):
+            gs = slice(first, first + count)
+            nc.vector.quantize_mx(
+                out=x_codes[m][:, gs].rearrange("p g r -> p (g r)").bitcast(FP8X4),
+                scales=x_scales[m][:, gs].rearrange("p g r -> p (g r)"),
+                in_=grouped[m][:, gs].rearrange("p g r t -> p (g r t)"),
+            )
+
+        uh_grouped = {}
+
+        def interleave_u_head(g, h, copy):
+            out = work.tile([P, HALF, 4], BF16, name="uh_grouped", tag="uh_grouped", align_bytes=64)
+            copy(
+                out=out[:].rearrange("p (c i) t -> p c t i", i=4),
+                in_=uh_raw[g][:, :, h * HALF : (h + 1) * HALF].rearrange("p t (c i) -> p c t i", i=4),
+            )
+            uh_grouped[g, h] = out
+
+        def quantize_u_head(g, h):
+            cols = slice(h * HALF, (h + 1) * HALF)
+            nc.vector.quantize_mx(
+                out=uh_codes[:, g, cols].bitcast(FP8X4),
+                scales=uh_scales[:, g, cols],
+                in_=uh_grouped[g, h][:].rearrange("p n t -> p (n t)"),
+            )
+
+        def multiply(m, g, h):
+            if (m, h) not in acc:
+                tag = "acc%d" % (2 * (m % 2) + h)
+                acc[m, h] = psum.tile([P, HALF], F32, name=tag, tag=tag)
+            cols = slice(h * HALF, (h + 1) * HALF)
+            if g < TAIL_PASSES:
+                rhs = ut_words[g // 2][:, g % 2, 2 * h * HALF : 2 * (h + 1) * HALF].bitcast(FP4X4)
+                rhs_scale = ut_scales[:, g, cols]
+            else:
+                rhs = uh_codes[:, g - TAIL_PASSES, cols].bitcast(FP8X4)
+                rhs_scale = uh_scales[:, g - TAIL_PASSES, cols]
+            nc.tensor.matmul_mx(
+                out=acc[m, h][:],
+                lhsT=x_codes[m][:, g, :].bitcast(FP8X4),
+                lhsT_scale=x_scales[m][:, g, :],
+                rhs=rhs,
+                rhs_scale=rhs_scale,
+                start=(g == 0),
+                stop=(g == PASSES - 1),
+            )
+
+        def multiply_passes(m, first, last):
+            for g in range(first, last):
+                for h in range(2):
+                    multiply(m, g, h)
+
+        def divide(m, h):
+            if m not in concepts:
+                concepts[m] = work.tile([P, N], F32, name="concepts", tag="concepts", bufs=6)
+                products[m] = work.tile([P, N], F32, name="products", tag="products", bufs=3)
+            cols = slice(h * HALF, (h + 1) * HALF)
+            nc.vector.tensor_tensor(out=concepts[m][:, cols], in0=acc[m, h][:], in1=inv_sigma[:, cols], op=MULT)
+
+        def finish(m):
+            for h in range(2):
+                cols = slice(h * HALF, (h + 1) * HALF)
+                divide(m, h)
+                nc.gpsimd.tensor_tensor(
+                    out=products[m][:, cols], in0=concepts[m][:, cols], in1=docs_sb[m][:, cols], op=MULT
+                )
+            nc.sync.dma_start(out=concepts_v[:, m, :], in_=concepts[m][:])
+
+        def sum_products(m):
+            nc.scalar.activation(out=products[m][:], in_=products[m][:], func=COPY, accum_out=scores[:, m : m + 1])
+
+        def turn_rows(dst, first, count):
+            bank = next_turn_bank()
+            for u in range(2):
+                nc.tensor.transpose(bank[:, u, 0, :], rows[:].bitcast(F32)[:, u:256:2], ident[:])
+            nc.vector.tensor_copy(out=dst[:], in_=bank[:, :, 0, first : first + count].rearrange("p u g -> p g u"))
+
+        nc.vector.memset(rows[:].bitcast(F32), 0.0)
+        make_identity(nc, ident[:])
+        nc.vector.memset(ut_scales[:].bitcast(I32), 0)
+
+        load_tf_tail(0, 0, 2)
+        nc.scalar.dma_start(out=rows[0:TAIL_PASSES, :], in_=idf_tail.rearrange("(g k) -> g k", k=K_PASS))
+        load_ut_words(0)
+        load_tf_tail(0, 2, 4)
+        scale_rows = u_tail_scales.rearrange("g (q r) n -> r q g n", r=4)
+        for r in range(4):
+            nc.sync.dma_start(out=ut_scales[r:P:32].bitcast(I32), in_=scale_rows[r].bitcast(I32))
+        load_ut_words(1)
+        load_tf_tail(1, 0, TAIL_PASSES)
+
+        turn_rows(idf_tail_words, 0, TAIL_PASSES)
+        nc.sync.dma_start(out=rows[6:8, :], in_=idf_head.rearrange("(g k) -> g k", k=K_PASS))
+        nc.sync.dma_start(out=rows[8:10, :], in_=sigma.rearrange("(g k) -> g k", k=K_PASS))
+        load_u_head(0)
+        load_ut_words(2)
+        load_tf_head(0)
+        load_u_head(1)
+        for m in range(2, TILES, 2):
+            load_tf_tail(m, 0, TAIL_PASSES)
+            load_tf_head(m)
+            load_tf_tail(m + 1, 0, TAIL_PASSES)
+            load_docs(m - 2)
+        load_docs(TILES - 2)
+
+        for m in range(2):
+            for pair in range(3):
+                turn(m, pair)
+            weigh(m, 0)
+            weigh(m, 1)
+            quantize_x(m, 0, 2)
+            weigh(m, 2)
+            quantize_x(m, 2, 2)
+            quantize_x(m, 4, 2)
+            multiply_passes(m, 0, 4)
+
+        turn_rows(late_words, 6, 4)
+        nc.vector.reciprocal(
+            out=inv_sigma_col[:], in_=late_words[:, 2:4, :].bitcast(BF16).rearrange("p h t -> p (h t)")
+        )
+        interleave_u_head(0, 0, nc.scalar.copy)
+        interleave_u_head(0, 1, nc.vector.tensor_copy)
+        multiply_passes(0, 4, 6)
+        for h in range(2):
+            bank = next_turn_bank()
+            spread = bank[:].rearrange("p a b n -> p (a b) n")
+            for t in range(4):
+                j = 4 * h + t
+                nc.tensor.transpose(spread[:, t, :], inv_sigma_col[:, j : j + 1].to_broadcast([P, P]), ident[:])
+            nc.scalar.copy(
+                out=inv_sigma[:, h * HALF : (h + 1) * HALF].rearrange("p (n t) -> p n t", t=4),
+                in_=spread.rearrange("p t n -> p n t"),
+            )
+        multiply_passes(1, 4, 6)
+        quantize_u_head(0, 1)
+        quantize_u_head(0, 0)
+
+        for m in range(2):
+            turn(m, 3)
+        for m in range(2):
+            weigh(m, 3)
+        for m in range(2):
+            quantize_x(m, 6, 2)
+        for m in range(2):
+            multiply_passes(m, 6, 7)
+        interleave_u_head(1, 0, nc.scalar.copy)
+        interleave_u_head(1, 1, nc.vector.tensor_copy)
+        quantize_u_head(1, 1)
+        quantize_u_head(1, 0)
+        for h in (1, 0):
+            for m in range(2):
+                multiply(m, 7, h)
+
+        for pair in range(PAIRS):
+            turn(2, pair)
+        sort_words(3)
+        finish(0)
+        weigh(2, 0)
+        weigh(2, 1)
+        weigh(2, 2)
+        quantize_x(2, 0, 4)
+        weigh(2, 3)
+        quantize_x(2, 4, 4)
+        multiply_passes(2, 0, 4)
+
+        for m in range(2, TILES - 1):
+            for pair in range(PAIRS):
+                turn(m + 1, pair)
+            if m + 2 < TILES:
+                sort_words(m + 2)
+            sum_products(m - 2)
+            finish(m - 1)
+            for pair in range(PAIRS):
+                weigh(m + 1, pair)
+            quantize_x(m + 1, 0, PASSES)
+            multiply_passes(m, 4 if m == 2 else 0, PASSES)
+
+        last = TILES - 1
+        sum_products(last - 2)
+        finish(last - 1)
+        sum_products(last - 1)
+        for h in range(2):
+            cols = slice(h * HALF, (h + 1) * HALF)
+            for g in range(PASSES):
+                multiply(last, g, h)
+            divide(last, h)
+            nc.sync.dma_start(out=concepts_v[:, last, cols], in_=concepts[last][:, cols])
+            nc.vector.scalar_tensor_tensor(
+                out=products[last][:, cols],
+                in0=concepts[last][:, cols],
+                scalar=1.0,
+                in1=docs_sb[last][:, cols],
+                op0=MULT,
+                op1=MULT,
+                accum_out=last_parts[:, h : h + 1],
+            )
+        nc.vector.tensor_tensor(out=scores[:, last : last + 1], in0=last_parts[:, 0:1], in1=last_parts[:, 1:2], op=ADD)
+        nc.sync.dma_start(out=scores_v, in_=scores[:])

@@ -46,37 +46,34 @@ def tile_lsi_query_fold_in_s1_kernel(
 
         ident = keep.tile([P, P], F32)
         rows = keep.tile([P, K_PASS], BF16)
-        idf_tail_words = keep.tile([P, TAIL_PASSES, 2], F32)
-        late_words = keep.tile([P, 4, 2], F32)
+        vec_words = keep.tile([P, PASSES + 2, 2], F32)
         inv_sigma_col = keep.tile([P, 8], F32)
         inv_sigma = keep.tile([P, N], F32)
         ut_scales = keep.tile([P, TAIL_PASSES, N], U8, align_bytes=64)
         uh_codes = keep.tile([P, HEAD_PASSES, N], U32, align_bytes=64)
         uh_scales = keep.tile([P, HEAD_PASSES, N], U8, align_bytes=64)
         scores = keep.tile([P, TILES], F32)
-        last_parts = keep.tile([P, 2], F32)
+        last_parts = keep.tile([P, 5], F32)
+        docs_over_sigma = keep.tile([P, N], F32)
 
         tf_words = {}
+        tf_runs = {}
         ut_words = {}
         uh_raw = {}
         docs_sb = {}
 
-        def load_tf_tail(m, first, count):
-            raw = keep.tile([P, count * K_PASS], BF16, name="tf_tail_%d_%d" % (m, first))
-            nc.sync.dma_start(out=raw[:], in_=tf_tail_v[:, m, first * K_PASS : (first + count) * K_PASS])
-            tf_words[m, first] = raw[:].bitcast(F32)
-            for g in range(first, first + count):
-                tf_words[m, g, "pass"] = raw[:].bitcast(F32)[:, (g - first) * 256 : (g - first + 1) * 256]
-
-        def load_tf_head(m):
-            raw = keep.tile([P, 2 * KH], BF16, name="tf_head_%d" % m)
-            nc.sync.dma_start(out=raw[:], in_=tf_head_v[:, m : m + 2, :].rearrange("p m k -> p (m k)"))
-            for i in range(2):
-                tf_words[m + i, TAIL_PASSES] = raw[:].bitcast(F32)[:, i * 512 : (i + 1) * 512]
-                for g in range(HEAD_PASSES):
-                    tf_words[m + i, TAIL_PASSES + g, "pass"] = raw[:].bitcast(F32)[
-                        :, i * 512 + g * 256 : i * 512 + (g + 1) * 256
-                    ]
+        def load_tf(source, m, tiles, first, count):
+            offset = first - TAIL_PASSES if first >= TAIL_PASSES else first
+            raw = keep.tile([P, tiles * count * K_PASS], BF16, name="tf_%d_%d" % (m, first))
+            nc.sync.dma_start(
+                out=raw[:].rearrange("p (m k) -> p m k", m=tiles),
+                in_=source[:, m : m + tiles, offset * K_PASS : (offset + count) * K_PASS],
+            )
+            words = raw[:].bitcast(F32).rearrange("p (m g w) -> p m g w", m=tiles, w=2 * P)
+            for i in range(tiles):
+                tf_runs[m + i, first] = words[:, i]
+                for g in range(count):
+                    tf_words[m + i, first + g] = words[:, i, g]
 
         def load_ut_words(pair):
             raw = keep.tile([P, 2, 2 * N], U8, name="ut_words_%d" % pair, align_bytes=64)
@@ -115,27 +112,26 @@ def tile_lsi_query_fold_in_s1_kernel(
         concepts = {}
         products = {}
 
-        def sort_words(m):
+        def sort_words(m, first, out):
+            run = tf_runs[m, first]
+            nc.scalar.copy(out=out, in_=run.rearrange("p g (w u) -> p g u w", u=2))
+            for g in range(run.shape[1]):
+                sorted_words[m, first + g] = out[:, g]
+
+        def sort_tile(m):
             out = work.tile([P, PASSES, 2, P], F32, name="sorted", tag="sorted")
-            nc.scalar.copy(
-                out=out[:, 0:TAIL_PASSES],
-                in_=tf_words[m, 0].rearrange("p (g w u) -> p g u w", u=2, w=P),
-            )
-            nc.scalar.copy(
-                out=out[:, TAIL_PASSES:PASSES],
-                in_=tf_words[m, TAIL_PASSES].rearrange("p (g w u) -> p g u w", u=2, w=P),
-            )
-            sorted_words[m] = out
+            sort_words(m, 0, out[:, :TAIL_PASSES])
+            sort_words(m, TAIL_PASSES, out[:, TAIL_PASSES:])
 
         def turn(m, pair):
             bank = next_turn_bank()
             for i in range(2):
                 g = 2 * pair + i
                 for u in range(2):
-                    if m in sorted_words:
-                        src = sorted_words[m][:, g, u, :]
+                    if (m, g) in sorted_words:
+                        src = sorted_words[m, g][:, u, :]
                     else:
-                        src = tf_words[m, g, "pass"][:, u:256:2]
+                        src = tf_words[m, g][:, u : 2 * P : 2]
                     nc.tensor.transpose(bank[:, u, i, :], src, ident[:])
             turned[m, pair] = bank
 
@@ -144,10 +140,7 @@ def tile_lsi_query_fold_in_s1_kernel(
                 grouped[m] = work.tile([P, PASSES, P, 4], BF16, name="grouped", tag="grouped", align_bytes=64)
                 x_codes[m] = work.tile([P, PASSES, P], U32, name="x_codes", tag="x_codes", bufs=3, align_bytes=64)
                 x_scales[m] = work.tile([P, PASSES, P], U8, name="x_scales", tag="x_scales", bufs=3, align_bytes=64)
-            if pair < PAIRS - 1:
-                idf = idf_tail_words[:, 2 * pair : 2 * pair + 2, :]
-            else:
-                idf = late_words[:, 0:2, :]
+            idf = vec_words[:, 2 * pair : 2 * pair + 2, :]
             idf = idf.bitcast(BF16).rearrange("p g (u e) -> p g u e", e=2).unsqueeze(2).broadcast_to([P, 2, P, 2, 2])
             nc.vector.tensor_tensor(
                 out=grouped[m][:, 2 * pair : 2 * pair + 2].rearrange("p g r (u e) -> p g r u e", e=2),
@@ -182,19 +175,15 @@ def tile_lsi_query_fold_in_s1_kernel(
                 in_=uh_grouped[g, h][:].rearrange("p n t -> p (n t)"),
             )
 
-        def multiply(m, g, h):
-            if (m, h) not in acc:
-                tag = "acc%d" % (2 * (m % 2) + h)
-                acc[m, h] = psum.tile([P, HALF], F32, name=tag, tag=tag)
-            cols = slice(h * HALF, (h + 1) * HALF)
+        def multiply_into(out, m, g, cols):
             if g < TAIL_PASSES:
-                rhs = ut_words[g // 2][:, g % 2, 2 * h * HALF : 2 * (h + 1) * HALF].bitcast(FP4X4)
+                rhs = ut_words[g // 2][:, g % 2, 2 * cols.start : 2 * cols.stop].bitcast(FP4X4)
                 rhs_scale = ut_scales[:, g, cols]
             else:
                 rhs = uh_codes[:, g - TAIL_PASSES, cols].bitcast(FP8X4)
                 rhs_scale = uh_scales[:, g - TAIL_PASSES, cols]
             nc.tensor.matmul_mx(
-                out=acc[m, h][:],
+                out=out,
                 lhsT=x_codes[m][:, g, :].bitcast(FP8X4),
                 lhsT_scale=x_scales[m][:, g, :],
                 rhs=rhs,
@@ -202,6 +191,15 @@ def tile_lsi_query_fold_in_s1_kernel(
                 start=(g == 0),
                 stop=(g == PASSES - 1),
             )
+
+        def acc_bank(m, h):
+            if (m, h) not in acc:
+                tag = "acc%d" % (2 * (m % 2) + h)
+                acc[m, h] = psum.tile([P, HALF], F32, name=tag, tag=tag)
+            return acc[m, h]
+
+        def multiply(m, g, h):
+            multiply_into(acc_bank(m, h)[:], m, g, slice(h * HALF, (h + 1) * HALF))
 
         def multiply_passes(m, first, last):
             for g in range(first, last):
@@ -227,58 +225,47 @@ def tile_lsi_query_fold_in_s1_kernel(
         def sum_products(m):
             nc.scalar.activation(out=products[m][:], in_=products[m][:], func=COPY, accum_out=scores[:, m : m + 1])
 
-        def turn_rows(dst, first, count):
-            bank = next_turn_bank()
-            for u in range(2):
-                nc.tensor.transpose(bank[:, u, 0, :], rows[:].bitcast(F32)[:, u:256:2], ident[:])
-            nc.vector.tensor_copy(out=dst[:], in_=bank[:, :, 0, first : first + count].rearrange("p u g -> p g u"))
-
         nc.vector.memset(rows[:].bitcast(F32), 0.0)
         make_identity(nc, ident[:])
         nc.vector.memset(ut_scales[:].bitcast(I32), 0)
 
-        load_tf_tail(0, 0, 2)
+        load_tf(tf_tail_v, 0, 2, 0, 2)
         nc.scalar.dma_start(out=rows[0:TAIL_PASSES, :], in_=idf_tail.rearrange("(g k) -> g k", k=K_PASS))
+        nc.scalar.dma_start(out=rows[6:8, :], in_=idf_head.rearrange("(g k) -> g k", k=K_PASS))
+        nc.scalar.dma_start(out=rows[8:10, :], in_=sigma.rearrange("(g k) -> g k", k=K_PASS))
         load_ut_words(0)
-        load_tf_tail(0, 2, 4)
+        load_tf(tf_tail_v, 0, 2, 2, 2)
         scale_rows = u_tail_scales.rearrange("g (q r) n -> r q g n", r=4)
         for r in range(4):
             nc.sync.dma_start(out=ut_scales[r:P:32].bitcast(I32), in_=scale_rows[r].bitcast(I32))
+        load_tf(tf_tail_v, 0, 2, 4, 2)
         load_ut_words(1)
-        load_tf_tail(1, 0, TAIL_PASSES)
-
-        turn_rows(idf_tail_words, 0, TAIL_PASSES)
-        nc.sync.dma_start(out=rows[6:8, :], in_=idf_head.rearrange("(g k) -> g k", k=K_PASS))
-        nc.sync.dma_start(out=rows[8:10, :], in_=sigma.rearrange("(g k) -> g k", k=K_PASS))
         load_u_head(0)
+        load_tf(tf_head_v, 0, 2, 6, 2)
         load_ut_words(2)
-        load_tf_head(0)
         load_u_head(1)
         for m in range(2, TILES, 2):
-            load_tf_tail(m, 0, TAIL_PASSES)
-            load_tf_head(m)
-            load_tf_tail(m + 1, 0, TAIL_PASSES)
+            load_tf(tf_tail_v, m, 1, 0, TAIL_PASSES)
+            load_tf(tf_head_v, m, 2, TAIL_PASSES, HEAD_PASSES)
+            load_tf(tf_tail_v, m + 1, 1, 0, TAIL_PASSES)
             load_docs(m - 2)
         load_docs(TILES - 2)
 
-        for m in range(2):
-            for pair in range(3):
-                turn(m, pair)
-            weigh(m, 0)
-            weigh(m, 1)
-            quantize_x(m, 0, 2)
-            weigh(m, 2)
-            quantize_x(m, 2, 2)
-            quantize_x(m, 4, 2)
-            multiply_passes(m, 0, 4)
-
-        turn_rows(late_words, 6, 4)
+        bank = next_turn_bank()
+        for u in range(2):
+            nc.tensor.transpose(bank[:, u, 0, :], rows[:].bitcast(F32)[:, u : 2 * P : 2], ident[:])
+        nc.vector.tensor_copy(out=vec_words[:], in_=bank[:, :, 0, 0 : PASSES + 2].rearrange("p u g -> p g u"))
         nc.vector.reciprocal(
-            out=inv_sigma_col[:], in_=late_words[:, 2:4, :].bitcast(BF16).rearrange("p h t -> p (h t)")
+            out=inv_sigma_col[:], in_=vec_words[:, PASSES:, :].bitcast(BF16).rearrange("p h t -> p (h t)")
         )
-        interleave_u_head(0, 0, nc.scalar.copy)
-        interleave_u_head(0, 1, nc.vector.tensor_copy)
-        multiply_passes(0, 4, 6)
+
+        def both(step, *args):
+            for m in range(2):
+                step(m, *args)
+
+        both(turn, 0)
+        both(weigh, 0)
+        both(quantize_x, 0, 2)
         for h in range(2):
             bank = next_turn_bank()
             spread = bank[:].rearrange("p a b n -> p (a b) n")
@@ -289,43 +276,51 @@ def tile_lsi_query_fold_in_s1_kernel(
                 out=inv_sigma[:, h * HALF : (h + 1) * HALF].rearrange("p (n t) -> p n t", t=4),
                 in_=spread.rearrange("p t n -> p n t"),
             )
-        multiply_passes(1, 4, 6)
+        both(turn, 1)
+        both(weigh, 1)
+        both(quantize_x, 2, 2)
+        early = work.tile([P, PASSES, 2, P], F32, name="sorted", tag="sorted")
+        for m in range(2):
+            sort_words(m, 4, early[:, 2 * m : 2 * m + 2])
+        both(multiply_passes, 0, 2)
+        both(turn, 2)
+        both(weigh, 2)
+        both(quantize_x, 4, 2)
+        both(multiply_passes, 2, 4)
+        interleave_u_head(0, 0, nc.scalar.copy)
+        interleave_u_head(0, 1, nc.vector.tensor_copy)
+        both(turn, 3)
+        weigh(0, 3)
         quantize_u_head(0, 1)
+        weigh(1, 3)
         quantize_u_head(0, 0)
-
-        for m in range(2):
-            turn(m, 3)
-        for m in range(2):
-            weigh(m, 3)
-        for m in range(2):
-            quantize_x(m, 6, 2)
-        for m in range(2):
-            multiply_passes(m, 6, 7)
+        both(quantize_x, 6, 2)
+        both(multiply_passes, 4, 6)
+        both(multiply_passes, 6, 7)
         interleave_u_head(1, 0, nc.scalar.copy)
         interleave_u_head(1, 1, nc.vector.tensor_copy)
+        for pair in range(PAIRS - 1):
+            turn(2, pair)
         quantize_u_head(1, 1)
         quantize_u_head(1, 0)
-        for h in (1, 0):
-            for m in range(2):
-                multiply(m, 7, h)
-
-        for pair in range(PAIRS):
-            turn(2, pair)
-        sort_words(3)
-        finish(0)
         weigh(2, 0)
         weigh(2, 1)
-        weigh(2, 2)
+        both(multiply_passes, 7, 8)
+        turn(2, PAIRS - 1)
+        sort_tile(3)
         quantize_x(2, 0, 4)
+        finish(0)
+        weigh(2, 2)
         weigh(2, 3)
-        quantize_x(2, 4, 4)
         multiply_passes(2, 0, 4)
+        quantize_x(2, 4, 4)
 
+        last = TILES - 1
         for m in range(2, TILES - 1):
             for pair in range(PAIRS):
                 turn(m + 1, pair)
             if m + 2 < TILES:
-                sort_words(m + 2)
+                sort_tile(m + 2)
             sum_products(m - 2)
             finish(m - 1)
             for pair in range(PAIRS):
@@ -333,24 +328,31 @@ def tile_lsi_query_fold_in_s1_kernel(
             quantize_x(m + 1, 0, PASSES)
             multiply_passes(m, 4 if m == 2 else 0, PASSES)
 
-        last = TILES - 1
+        nc.vector.tensor_tensor(out=docs_over_sigma[:], in0=inv_sigma[:], in1=docs_sb[last], op=MULT)
         sum_products(last - 2)
         finish(last - 1)
         sum_products(last - 1)
-        for h in range(2):
-            cols = slice(h * HALF, (h + 1) * HALF)
+        concepts_last = work.tile([P, N], F32, name="concepts", tag="concepts", bufs=6)
+        products_last = work.tile([P, N], F32, name="products", tag="products", bufs=3)
+        parts = [slice(0, HALF)] + [slice(c, c + P) for c in range(HALF, N, P)]
+        stored = 0
+        for part, cols in enumerate(parts):
+            sums = acc_bank(last, 0)[:] if part == 0 else next_turn_bank()[:, 0, 0, :]
             for g in range(PASSES):
-                multiply(last, g, h)
-            divide(last, h)
-            nc.sync.dma_start(out=concepts_v[:, last, cols], in_=concepts[last][:, cols])
+                multiply_into(sums, last, g, cols)
             nc.vector.scalar_tensor_tensor(
-                out=products[last][:, cols],
-                in0=concepts[last][:, cols],
+                out=products_last[:, cols],
+                in0=sums,
                 scalar=1.0,
-                in1=docs_sb[last][:, cols],
+                in1=docs_over_sigma[:, cols],
                 op0=MULT,
                 op1=MULT,
-                accum_out=last_parts[:, h : h + 1],
+                accum_out=last_parts[:, part : part + 1],
             )
-        nc.vector.tensor_tensor(out=scores[:, last : last + 1], in0=last_parts[:, 0:1], in1=last_parts[:, 1:2], op=ADD)
-        nc.sync.dma_start(out=scores_v, in_=scores[:])
+            nc.vector.tensor_tensor(out=concepts_last[:, cols], in0=sums, in1=inv_sigma[:, cols], op=MULT)
+            if part % 2 == 0:
+                ready = slice(stored, cols.stop)
+                nc.sync.dma_start(out=concepts_v[:, last, ready], in_=concepts_last[:, ready])
+                stored = cols.stop
+        nc.vector.reduce_sum(out=scores[:, last : last + 1], in_=last_parts[:], axis=mybir.AxisListType.X)
+        nc.scalar.dma_start(out=scores_v, in_=scores[:])

@@ -26,6 +26,7 @@ TILES = M // P
 HALF = 512
 PAIRS = PASSES // 2
 TURN_BANKS = 4
+WARMUPS = 5
 
 
 def tile_lsi_query_fold_in_s1_kernel(
@@ -213,6 +214,9 @@ def tile_lsi_query_fold_in_s1_kernel(
             cols = slice(h * HALF, (h + 1) * HALF)
             nc.vector.tensor_tensor(out=concepts[m][:, cols], in0=acc[m, h][:], in1=inv_sigma[:, cols], op=MULT)
 
+        def store_concepts(m):
+            nc.sync.dma_start(out=concepts_v[:, m, :], in_=concepts[m][:])
+
         def finish(m):
             for h in range(2):
                 cols = slice(h * HALF, (h + 1) * HALF)
@@ -220,12 +224,25 @@ def tile_lsi_query_fold_in_s1_kernel(
                 nc.gpsimd.tensor_tensor(
                     out=products[m][:, cols], in0=concepts[m][:, cols], in1=docs_sb[m][:, cols], op=MULT
                 )
-            nc.sync.dma_start(out=concepts_v[:, m, :], in_=concepts[m][:])
+            store_concepts(m)
+
+        def score_on_vector(m):
+            nc.vector.scalar_tensor_tensor(
+                out=products[m][:],
+                in0=concepts[m][:],
+                scalar=1.0,
+                in1=docs_sb[m],
+                op0=MULT,
+                op1=MULT,
+                accum_out=scores[:, m : m + 1],
+            )
 
         def sum_products(m):
             nc.scalar.activation(out=products[m][:], in_=products[m][:], func=COPY, accum_out=scores[:, m : m + 1])
 
         nc.vector.memset(rows[:].bitcast(F32), 0.0)
+        zeros = keep.tile([P, HALF], BF16)
+        nc.vector.memset(zeros[:].bitcast(F32), 0.0)
         make_identity(nc, ident[:])
         nc.vector.memset(ut_scales[:].bitcast(I32), 0)
 
@@ -251,6 +268,9 @@ def tile_lsi_query_fold_in_s1_kernel(
             load_docs(m - 2)
         load_docs(TILES - 2)
 
+        warm = next_turn_bank()
+        for i in range(WARMUPS):
+            nc.tensor.matmul(warm[:].rearrange("p a b n -> p (a b n)"), zeros[:, :P], zeros[:], start=True, stop=True)
         bank = next_turn_bank()
         for u in range(2):
             nc.tensor.transpose(bank[:, u, 0, :], rows[:].bitcast(F32)[:, u : 2 * P : 2], ident[:])
@@ -259,6 +279,18 @@ def tile_lsi_query_fold_in_s1_kernel(
             out=inv_sigma_col[:], in_=vec_words[:, PASSES:, :].bitcast(BF16).rearrange("p h t -> p (h t)")
         )
 
+        def spread_inv_sigma(h):
+            spread = next_turn_bank()[:].rearrange("p a b n -> p (a b) n")
+            for t in range(4):
+                j = 4 * h + t
+                nc.tensor.matmul(
+                    spread[:, t, :], inv_sigma_col[:, j : j + 1].to_broadcast([P, P]), ident[:], start=True, stop=True
+                )
+            nc.scalar.copy(
+                out=inv_sigma[:, h * HALF : (h + 1) * HALF].rearrange("p (n t) -> p n t", t=4),
+                in_=spread.rearrange("p t n -> p n t"),
+            )
+
         def both(step, *args):
             for m in range(2):
                 step(m, *args)
@@ -266,17 +298,9 @@ def tile_lsi_query_fold_in_s1_kernel(
         both(turn, 0)
         both(weigh, 0)
         both(quantize_x, 0, 2)
-        for h in range(2):
-            bank = next_turn_bank()
-            spread = bank[:].rearrange("p a b n -> p (a b) n")
-            for t in range(4):
-                j = 4 * h + t
-                nc.tensor.transpose(spread[:, t, :], inv_sigma_col[:, j : j + 1].to_broadcast([P, P]), ident[:])
-            nc.scalar.copy(
-                out=inv_sigma[:, h * HALF : (h + 1) * HALF].rearrange("p (n t) -> p n t", t=4),
-                in_=spread.rearrange("p t n -> p n t"),
-            )
+        spread_inv_sigma(0)
         both(turn, 1)
+        spread_inv_sigma(1)
         both(weigh, 1)
         both(quantize_x, 2, 2)
         early = work.tile([P, PASSES, 2, P], F32, name="sorted", tag="sorted")
@@ -299,20 +323,26 @@ def tile_lsi_query_fold_in_s1_kernel(
         both(multiply_passes, 6, 7)
         interleave_u_head(1, 0, nc.scalar.copy)
         interleave_u_head(1, 1, nc.vector.tensor_copy)
-        for pair in range(PAIRS - 1):
-            turn(2, pair)
+        turn(2, 0)
+        turn(2, 1)
         quantize_u_head(1, 1)
         quantize_u_head(1, 0)
         weigh(2, 0)
         weigh(2, 1)
-        both(multiply_passes, 7, 8)
-        turn(2, PAIRS - 1)
+        both(multiply, 7, 1)
+        both(multiply, 7, 0)
+        turn(2, 2)
+        turn(2, 3)
         sort_tile(3)
+        divide(0, 1)
         quantize_x(2, 0, 4)
-        finish(0)
+        divide(0, 0)
+        store_concepts(0)
         weigh(2, 2)
         weigh(2, 3)
-        multiply_passes(2, 0, 4)
+        for h in (1, 0):
+            for g in range(4):
+                multiply(2, g, h)
         quantize_x(2, 4, 4)
 
         last = TILES - 1
@@ -321,17 +351,22 @@ def tile_lsi_query_fold_in_s1_kernel(
                 turn(m + 1, pair)
             if m + 2 < TILES:
                 sort_tile(m + 2)
-            sum_products(m - 2)
+            if m > 2:
+                sum_products(m - 2)
             finish(m - 1)
             for pair in range(PAIRS):
                 weigh(m + 1, pair)
             quantize_x(m + 1, 0, PASSES)
+            if m == 3:
+                score_on_vector(0)
             multiply_passes(m, 4 if m == 2 else 0, PASSES)
 
         nc.vector.tensor_tensor(out=docs_over_sigma[:], in0=inv_sigma[:], in1=docs_sb[last], op=MULT)
         sum_products(last - 2)
-        finish(last - 1)
-        sum_products(last - 1)
+        divide(last - 1, 0)
+        divide(last - 1, 1)
+        store_concepts(last - 1)
+        score_on_vector(last - 1)
         concepts_last = work.tile([P, N], F32, name="concepts", tag="concepts", bufs=6)
         products_last = work.tile([P, N], F32, name="products", tag="products", bufs=3)
         parts = [slice(0, HALF)] + [slice(c, c + P) for c in range(HALF, N, P)]

@@ -14,19 +14,25 @@ U8 = mybir.dt.uint8
 FP8X4 = mybir.dt.float8_e4m3fn_x4
 FP4X4 = mybir.dt.float4_e2m1fn_x4
 MULT = mybir.AluOpType.mult
-ADD = mybir.AluOpType.add
 COPY = mybir.ActivationFunctionType.Copy
 
 P = 128
-K_PASS = 512
+PACK = 4
+K_PASS = P * PACK
+WORDS = K_PASS // 2
 TAIL_PASSES = KT // K_PASS
 HEAD_PASSES = KH // K_PASS
 PASSES = TAIL_PASSES + HEAD_PASSES
-TILES = M // P
-HALF = 512
 PAIRS = PASSES // 2
+TILES = M // P
+LAST = TILES - 1
+HALF = 512
+SIGMA_ROWS = N // K_PASS
 TURN_BANKS = 4
-WARMUPS = 5
+CONCEPT_BUFS = 6
+PRODUCT_BUFS = 4
+SCORE_FIRST_TILE_IN = 4
+SCALE_LAST_DOCS_IN = 5
 
 
 def tile_lsi_query_fold_in_s1_kernel(
@@ -46,50 +52,69 @@ def tile_lsi_query_fold_in_s1_kernel(
         ctx.enter_context(tc.manual_schedule())
 
         ident = keep.tile([P, P], F32)
-        rows = keep.tile([P, K_PASS], BF16)
-        vec_words = keep.tile([P, PASSES + 2, 2], F32)
-        inv_sigma_col = keep.tile([P, 8], F32)
+        vec_rows = keep.tile([P, K_PASS], BF16)
+        vec_words = keep.tile([P, PASSES + SIGMA_ROWS, 2], F32)
+        inv_sigma_cols = keep.tile([P, SIGMA_ROWS * PACK], F32)
         inv_sigma = keep.tile([P, N], F32)
         ut_scales = keep.tile([P, TAIL_PASSES, N], U8, align_bytes=64)
         uh_codes = keep.tile([P, HEAD_PASSES, N], U32, align_bytes=64)
         uh_scales = keep.tile([P, HEAD_PASSES, N], U8, align_bytes=64)
         scores = keep.tile([P, TILES], F32)
-        last_parts = keep.tile([P, 5], F32)
-        docs_over_sigma = keep.tile([P, N], F32)
+        last_parts = [slice(0, HALF)] + [slice(c, c + P) for c in range(HALF, N, P)]
+        last_part_scores = keep.tile([P, len(last_parts)], F32)
+        last_docs_over_sigma = keep.tile([P, N], F32)
 
-        tf_words = {}
         tf_runs = {}
+        tf_words = {}
+        sorted_words = {}
+        turned = {}
+        x_bf16 = {}
+        x_codes = {}
+        x_scales = {}
         ut_words = {}
-        uh_raw = {}
+        uh_rows = {}
+        uh_bf16 = {}
         docs_sb = {}
+        sums = {}
+        concepts = {}
+        products = {}
+        turn_banks_taken = []
 
-        def load_tf(source, m, tiles, first, count):
-            offset = first - TAIL_PASSES if first >= TAIL_PASSES else first
+        def half_cols(h):
+            return slice(h * HALF, (h + 1) * HALF)
+
+
+        def load_tf(m, tiles, first, count):
+            source, start = (tf_tail_v, first) if first < TAIL_PASSES else (tf_head_v, first - TAIL_PASSES)
             raw = keep.tile([P, tiles * count * K_PASS], BF16, name="tf_%d_%d" % (m, first))
             nc.sync.dma_start(
                 out=raw[:].rearrange("p (m k) -> p m k", m=tiles),
-                in_=source[:, m : m + tiles, offset * K_PASS : (offset + count) * K_PASS],
+                in_=source[:, m : m + tiles, start * K_PASS : (start + count) * K_PASS],
             )
-            words = raw[:].bitcast(F32).rearrange("p (m g w) -> p m g w", m=tiles, w=2 * P)
+            words = raw[:].bitcast(F32).rearrange("p (m g w) -> p m g w", m=tiles, w=WORDS)
             for i in range(tiles):
                 tf_runs[m + i, first] = words[:, i]
                 for g in range(count):
                     tf_words[m + i, first + g] = words[:, i, g]
 
         def load_ut_words(pair):
-            raw = keep.tile([P, 2, 2 * N], U8, name="ut_words_%d" % pair, align_bytes=64)
+            ut_words[pair] = keep.tile([P, 2, 2 * N], U8, name="ut_words_%d" % pair, align_bytes=64)
             nc.sync.dma_start(
-                out=raw[:].bitcast(I32),
+                out=ut_words[pair][:].bitcast(I32),
                 in_=u_tail_words[2 * pair : 2 * pair + 2].rearrange("g p n -> p g n").bitcast(I32),
             )
-            ut_words[pair] = raw
+
+        def load_ut_scales():
+            by_row = u_tail_scales.rearrange("g (q r) n -> r q g n", r=4)
+            for r in range(4):
+                nc.sync.dma_start(out=ut_scales[r:P:32].bitcast(I32), in_=by_row[r].bitcast(I32))
 
         def load_u_head(g):
-            raw = keep.tile([P, 4, N], BF16, name="u_head_%d" % g)
+            uh_rows[g] = keep.tile([P, PACK, N], BF16, name="u_head_%d" % g)
             nc.sync.dma_start(
-                out=raw[:], in_=u_head[g * K_PASS : (g + 1) * K_PASS, :].rearrange("(p t) n -> p t n", t=4)
+                out=uh_rows[g][:],
+                in_=u_head[g * K_PASS : (g + 1) * K_PASS, :].rearrange("(p t) n -> p t n", t=PACK),
             )
-            uh_raw[g] = raw
 
         def load_docs(m):
             raw = keep.tile([P, 2, N], BF16, name="docs_%d" % m)
@@ -97,21 +122,11 @@ def tile_lsi_query_fold_in_s1_kernel(
             docs_sb[m] = raw[:, 0, :]
             docs_sb[m + 1] = raw[:, 1, :]
 
-        turn_count = []
 
         def next_turn_bank():
-            tag = "turn%d" % (len(turn_count) % TURN_BANKS)
-            turn_count.append(tag)
+            tag = "turn%d" % (len(turn_banks_taken) % TURN_BANKS)
+            turn_banks_taken.append(tag)
             return psum.tile([P, 2, 2, P], F32, name=tag, tag=tag)
-
-        sorted_words = {}
-        turned = {}
-        grouped = {}
-        x_codes = {}
-        x_scales = {}
-        acc = {}
-        concepts = {}
-        products = {}
 
         def sort_words(m, first, out):
             run = tf_runs[m, first]
@@ -125,56 +140,50 @@ def tile_lsi_query_fold_in_s1_kernel(
             sort_words(m, TAIL_PASSES, out[:, TAIL_PASSES:])
 
         def turn(m, pair):
-            bank = next_turn_bank()
+            turned[m, pair] = next_turn_bank()
             for i in range(2):
                 g = 2 * pair + i
                 for u in range(2):
-                    if (m, g) in sorted_words:
-                        src = sorted_words[m, g][:, u, :]
-                    else:
-                        src = tf_words[m, g][:, u : 2 * P : 2]
-                    nc.tensor.transpose(bank[:, u, i, :], src, ident[:])
-            turned[m, pair] = bank
+                    words = sorted_words[m, g][:, u, :] if (m, g) in sorted_words else tf_words[m, g][:, u:WORDS:2]
+                    nc.tensor.transpose(turned[m, pair][:, u, i, :], words, ident[:])
 
         def weigh(m, pair):
-            if m not in grouped:
-                grouped[m] = work.tile([P, PASSES, P, 4], BF16, name="grouped", tag="grouped", align_bytes=64)
+            if m not in x_bf16:
+                x_bf16[m] = work.tile([P, PASSES, P, PACK], BF16, name="x_bf16", tag="x_bf16", align_bytes=64)
                 x_codes[m] = work.tile([P, PASSES, P], U32, name="x_codes", tag="x_codes", bufs=3, align_bytes=64)
                 x_scales[m] = work.tile([P, PASSES, P], U8, name="x_scales", tag="x_scales", bufs=3, align_bytes=64)
-            idf = vec_words[:, 2 * pair : 2 * pair + 2, :]
-            idf = idf.bitcast(BF16).rearrange("p g (u e) -> p g u e", e=2).unsqueeze(2).broadcast_to([P, 2, P, 2, 2])
+            both_passes = slice(2 * pair, 2 * pair + 2)
+            idf = vec_words[:, both_passes, :].bitcast(BF16).rearrange("p g (u e) -> p g u e", e=2)
             nc.vector.tensor_tensor(
-                out=grouped[m][:, 2 * pair : 2 * pair + 2].rearrange("p g r (u e) -> p g r u e", e=2),
+                out=x_bf16[m][:, both_passes].rearrange("p g r (u e) -> p g r u e", e=2),
                 in0=turned[m, pair][:].bitcast(BF16).rearrange("p u g (r e) -> p g r u e", e=2),
-                in1=idf,
+                in1=idf.unsqueeze(2).broadcast_to([P, 2, P, 2, 2]),
                 op=MULT,
             )
 
         def quantize_x(m, first, count):
-            gs = slice(first, first + count)
+            passes = slice(first, first + count)
             nc.vector.quantize_mx(
-                out=x_codes[m][:, gs].rearrange("p g r -> p (g r)").bitcast(FP8X4),
-                scales=x_scales[m][:, gs].rearrange("p g r -> p (g r)"),
-                in_=grouped[m][:, gs].rearrange("p g r t -> p (g r t)"),
+                out=x_codes[m][:, passes].rearrange("p g r -> p (g r)").bitcast(FP8X4),
+                scales=x_scales[m][:, passes].rearrange("p g r -> p (g r)"),
+                in_=x_bf16[m][:, passes].rearrange("p g r t -> p (g r t)"),
             )
 
-        uh_grouped = {}
 
         def interleave_u_head(g, h, copy):
-            out = work.tile([P, HALF, 4], BF16, name="uh_grouped", tag="uh_grouped", align_bytes=64)
+            uh_bf16[g, h] = work.tile([P, HALF, PACK], BF16, name="uh_bf16", tag="uh_bf16", align_bytes=64)
             copy(
-                out=out[:].rearrange("p (c i) t -> p c t i", i=4),
-                in_=uh_raw[g][:, :, h * HALF : (h + 1) * HALF].rearrange("p t (c i) -> p c t i", i=4),
+                out=uh_bf16[g, h][:].rearrange("p (c i) t -> p c t i", i=4),
+                in_=uh_rows[g][:, :, half_cols(h)].rearrange("p t (c i) -> p c t i", i=4),
             )
-            uh_grouped[g, h] = out
 
         def quantize_u_head(g, h):
-            cols = slice(h * HALF, (h + 1) * HALF)
             nc.vector.quantize_mx(
-                out=uh_codes[:, g, cols].bitcast(FP8X4),
-                scales=uh_scales[:, g, cols],
-                in_=uh_grouped[g, h][:].rearrange("p n t -> p (n t)"),
+                out=uh_codes[:, g, half_cols(h)].bitcast(FP8X4),
+                scales=uh_scales[:, g, half_cols(h)],
+                in_=uh_bf16[g, h][:].rearrange("p n t -> p (n t)"),
             )
+
 
         def multiply_into(out, m, g, cols):
             if g < TAIL_PASSES:
@@ -193,134 +202,124 @@ def tile_lsi_query_fold_in_s1_kernel(
                 stop=(g == PASSES - 1),
             )
 
-        def acc_bank(m, h):
-            if (m, h) not in acc:
-                tag = "acc%d" % (2 * (m % 2) + h)
-                acc[m, h] = psum.tile([P, HALF], F32, name=tag, tag=tag)
-            return acc[m, h]
+        def sum_bank(m, h):
+            if (m, h) not in sums:
+                tag = "sums%d" % (2 * (m % 2) + h)
+                sums[m, h] = psum.tile([P, HALF], F32, name=tag, tag=tag)
+            return sums[m, h]
 
         def multiply(m, g, h):
-            multiply_into(acc_bank(m, h)[:], m, g, slice(h * HALF, (h + 1) * HALF))
+            multiply_into(sum_bank(m, h)[:], m, g, half_cols(h))
 
-        def multiply_passes(m, first, last):
-            for g in range(first, last):
+        def multiply_passes(m, first, stop):
+            for g in range(first, stop):
                 for h in range(2):
                     multiply(m, g, h)
 
-        def divide(m, h):
-            if m not in concepts:
-                concepts[m] = work.tile([P, N], F32, name="concepts", tag="concepts", bufs=6)
-                products[m] = work.tile([P, N], F32, name="products", tag="products", bufs=3)
-            cols = slice(h * HALF, (h + 1) * HALF)
-            nc.vector.tensor_tensor(out=concepts[m][:, cols], in0=acc[m, h][:], in1=inv_sigma[:, cols], op=MULT)
 
-        def store_concepts(m):
-            nc.sync.dma_start(out=concepts_v[:, m, :], in_=concepts[m][:])
+        def new_output_tiles(m):
+            concepts[m] = work.tile([P, N], F32, name="concepts", tag="concepts", bufs=CONCEPT_BUFS)
+            products[m] = work.tile([P, N], F32, name="products", tag="products", bufs=PRODUCT_BUFS)
+
+        def divide(m, cols, bank):
+            nc.vector.tensor_tensor(out=concepts[m][:, cols], in0=bank, in1=inv_sigma[:, cols], op=MULT)
+
+        def store_concepts(m, cols):
+            nc.sync.dma_start(out=concepts_v[:, m, cols], in_=concepts[m][:, cols])
 
         def finish(m):
+            new_output_tiles(m)
             for h in range(2):
-                cols = slice(h * HALF, (h + 1) * HALF)
-                divide(m, h)
+                cols = half_cols(h)
+                divide(m, cols, sums[m, h][:])
                 nc.gpsimd.tensor_tensor(
                     out=products[m][:, cols], in0=concepts[m][:, cols], in1=docs_sb[m][:, cols], op=MULT
                 )
-            store_concepts(m)
-
-        def score_on_vector(m):
-            nc.vector.scalar_tensor_tensor(
-                out=products[m][:],
-                in0=concepts[m][:],
-                scalar=1.0,
-                in1=docs_sb[m],
-                op0=MULT,
-                op1=MULT,
-                accum_out=scores[:, m : m + 1],
-            )
+            store_concepts(m, slice(0, N))
 
         def sum_products(m):
             nc.scalar.activation(out=products[m][:], in_=products[m][:], func=COPY, accum_out=scores[:, m : m + 1])
 
-        nc.vector.memset(rows[:].bitcast(F32), 0.0)
-        zeros = keep.tile([P, HALF], BF16)
-        nc.vector.memset(zeros[:].bitcast(F32), 0.0)
-        make_identity(nc, ident[:])
-        nc.vector.memset(ut_scales[:].bitcast(I32), 0)
-
-        load_tf(tf_tail_v, 0, 2, 0, 2)
-        nc.scalar.dma_start(out=rows[0:TAIL_PASSES, :], in_=idf_tail.rearrange("(g k) -> g k", k=K_PASS))
-        nc.scalar.dma_start(out=rows[6:8, :], in_=idf_head.rearrange("(g k) -> g k", k=K_PASS))
-        nc.scalar.dma_start(out=rows[8:10, :], in_=sigma.rearrange("(g k) -> g k", k=K_PASS))
-        load_ut_words(0)
-        load_tf(tf_tail_v, 0, 2, 2, 2)
-        scale_rows = u_tail_scales.rearrange("g (q r) n -> r q g n", r=4)
-        for r in range(4):
-            nc.sync.dma_start(out=ut_scales[r:P:32].bitcast(I32), in_=scale_rows[r].bitcast(I32))
-        load_tf(tf_tail_v, 0, 2, 4, 2)
-        load_ut_words(1)
-        load_u_head(0)
-        load_tf(tf_head_v, 0, 2, 6, 2)
-        load_ut_words(2)
-        load_u_head(1)
-        for m in range(2, TILES, 2):
-            load_tf(tf_tail_v, m, 1, 0, TAIL_PASSES)
-            load_tf(tf_head_v, m, 2, TAIL_PASSES, HEAD_PASSES)
-            load_tf(tf_tail_v, m + 1, 1, 0, TAIL_PASSES)
-            load_docs(m - 2)
-        load_docs(TILES - 2)
-
-        warm = next_turn_bank()
-        for i in range(WARMUPS):
-            nc.tensor.matmul(warm[:].rearrange("p a b n -> p (a b n)"), zeros[:, :P], zeros[:], start=True, stop=True)
-        bank = next_turn_bank()
-        for u in range(2):
-            nc.tensor.transpose(bank[:, u, 0, :], rows[:].bitcast(F32)[:, u : 2 * P : 2], ident[:])
-        nc.vector.tensor_copy(out=vec_words[:], in_=bank[:, :, 0, 0 : PASSES + 2].rearrange("p u g -> p g u"))
-        nc.vector.reciprocal(
-            out=inv_sigma_col[:], in_=vec_words[:, PASSES:, :].bitcast(BF16).rearrange("p h t -> p (h t)")
-        )
+        def multiply_and_sum(out, in0, in1, total):
+            nc.vector.scalar_tensor_tensor(out=out, in0=in0, scalar=1.0, in1=in1, op0=MULT, op1=MULT, accum_out=total)
 
         def spread_inv_sigma(h):
             spread = next_turn_bank()[:].rearrange("p a b n -> p (a b) n")
-            for t in range(4):
-                j = 4 * h + t
-                nc.tensor.matmul(
-                    spread[:, t, :], inv_sigma_col[:, j : j + 1].to_broadcast([P, P]), ident[:], start=True, stop=True
-                )
+            for t in range(PACK):
+                column = inv_sigma_cols[:, PACK * h + t : PACK * h + t + 1]
+                nc.tensor.transpose(spread[:, t, :], column.to_broadcast([P, P]), ident[:])
             nc.scalar.copy(
-                out=inv_sigma[:, h * HALF : (h + 1) * HALF].rearrange("p (n t) -> p n t", t=4),
+                out=inv_sigma[:, half_cols(h)].rearrange("p (n t) -> p n t", t=PACK),
                 in_=spread.rearrange("p t n -> p n t"),
             )
 
-        def both(step, *args):
-            for m in range(2):
-                step(m, *args)
+        def first_two(step, *args):
+            step(0, *args)
+            step(1, *args)
 
-        both(turn, 0)
-        both(weigh, 0)
-        both(quantize_x, 0, 2)
+        nc.vector.memset(vec_rows[:].bitcast(F32), 0.0)
+        make_identity(nc, ident[:])
+        nc.vector.memset(ut_scales[:].bitcast(I32), 0)
+
+        load_tf(0, 2, 0, 2)
+        nc.scalar.dma_start(out=vec_rows[:TAIL_PASSES], in_=idf_tail.rearrange("(g k) -> g k", k=K_PASS))
+        nc.scalar.dma_start(out=vec_rows[TAIL_PASSES:PASSES], in_=idf_head.rearrange("(g k) -> g k", k=K_PASS))
+        nc.scalar.dma_start(
+            out=vec_rows[PASSES : PASSES + SIGMA_ROWS], in_=sigma.rearrange("(h k) -> h k", k=K_PASS)
+        )
+        load_ut_words(0)
+        load_tf(0, 2, 2, 2)
+        load_ut_scales()
+        load_tf(0, 2, 4, 2)
+        load_ut_words(1)
+        load_u_head(0)
+        load_tf(0, 2, TAIL_PASSES, HEAD_PASSES)
+        load_ut_words(2)
+        load_u_head(1)
+        for m in range(2, TILES, 2):
+            load_tf(m, 1, 0, TAIL_PASSES)
+            load_tf(m, 2, TAIL_PASSES, HEAD_PASSES)
+            load_tf(m + 1, 1, 0, TAIL_PASSES)
+            load_docs(m - 2)
+        load_docs(TILES - 2)
+
+        vec_bank = next_turn_bank()
+        for u in range(2):
+            nc.tensor.transpose(vec_bank[:, u, 0, :], vec_rows[:].bitcast(F32)[:, u:WORDS:2], ident[:])
+        nc.vector.tensor_copy(
+            out=vec_words[:], in_=vec_bank[:, :, 0, : PASSES + SIGMA_ROWS].rearrange("p u g -> p g u")
+        )
+        nc.vector.reciprocal(
+            out=inv_sigma_cols[:], in_=vec_words[:, PASSES:, :].bitcast(BF16).rearrange("p h t -> p (h t)")
+        )
+
+        first_two(turn, 0)
+        first_two(weigh, 0)
+        first_two(quantize_x, 0, 2)
         spread_inv_sigma(0)
-        both(turn, 1)
+        first_two(turn, 1)
         spread_inv_sigma(1)
-        both(weigh, 1)
-        both(quantize_x, 2, 2)
-        early = work.tile([P, PASSES, 2, P], F32, name="sorted", tag="sorted")
+        first_two(weigh, 1)
+        first_two(quantize_x, 2, 2)
+        sorted_pair = work.tile([P, 2, 2, 2, P], F32, name="sorted", tag="sorted")
         for m in range(2):
-            sort_words(m, 4, early[:, 2 * m : 2 * m + 2])
-        both(multiply_passes, 0, 2)
-        both(turn, 2)
-        both(weigh, 2)
-        both(quantize_x, 4, 2)
-        both(multiply_passes, 2, 4)
+            sort_words(m, 4, sorted_pair[:, m])
+        first_two(multiply_passes, 0, 2)
+        first_two(turn, 2)
+        first_two(weigh, 2)
+        first_two(quantize_x, 4, 2)
+        first_two(multiply_passes, 2, 4)
         interleave_u_head(0, 0, nc.scalar.copy)
         interleave_u_head(0, 1, nc.vector.tensor_copy)
-        both(turn, 3)
+        first_two(turn, 3)
         weigh(0, 3)
         quantize_u_head(0, 1)
         weigh(1, 3)
         quantize_u_head(0, 0)
-        both(quantize_x, 6, 2)
-        both(multiply_passes, 4, 6)
-        both(multiply_passes, 6, 7)
+        first_two(quantize_x, 6, 2)
+        first_two(multiply_passes, 4, 6)
+        first_two(multiply_passes, 6, 7)
+
         interleave_u_head(1, 0, nc.scalar.copy)
         interleave_u_head(1, 1, nc.vector.tensor_copy)
         turn(2, 0)
@@ -329,24 +328,24 @@ def tile_lsi_query_fold_in_s1_kernel(
         quantize_u_head(1, 0)
         weigh(2, 0)
         weigh(2, 1)
-        both(multiply, 7, 1)
-        both(multiply, 7, 0)
+        first_two(multiply, PASSES - 1, 1)
+        first_two(multiply, PASSES - 1, 0)
         turn(2, 2)
         turn(2, 3)
         sort_tile(3)
-        divide(0, 1)
-        quantize_x(2, 0, 4)
-        divide(0, 0)
-        store_concepts(0)
+        new_output_tiles(0)
+        divide(0, half_cols(1), sums[0, 1][:])
+        quantize_x(2, 0, PASSES // 2)
+        divide(0, half_cols(0), sums[0, 0][:])
+        store_concepts(0, slice(0, N))
         weigh(2, 2)
         weigh(2, 3)
         for h in (1, 0):
-            for g in range(4):
+            for g in range(PASSES // 2):
                 multiply(2, g, h)
-        quantize_x(2, 4, 4)
+        quantize_x(2, PASSES // 2, PASSES // 2)
 
-        last = TILES - 1
-        for m in range(2, TILES - 1):
+        for m in range(2, LAST):
             for pair in range(PAIRS):
                 turn(m + 1, pair)
             if m + 2 < TILES:
@@ -356,38 +355,30 @@ def tile_lsi_query_fold_in_s1_kernel(
             finish(m - 1)
             for pair in range(PAIRS):
                 weigh(m + 1, pair)
-            quantize_x(m + 1, 0, PASSES)
-            if m == 3:
-                score_on_vector(0)
-            multiply_passes(m, 4 if m == 2 else 0, PASSES)
+            quantize_x(m + 1, 0, PASSES // 2)
+            quantize_x(m + 1, PASSES // 2, PASSES // 2)
+            if m == SCORE_FIRST_TILE_IN:
+                multiply_and_sum(products[0][:], concepts[0][:], docs_sb[0], scores[:, 0:1])
+            if m == SCALE_LAST_DOCS_IN:
+                nc.vector.tensor_tensor(out=last_docs_over_sigma[:], in0=inv_sigma[:], in1=docs_sb[LAST], op=MULT)
+            multiply_passes(m, PASSES // 2 if m == 2 else 0, PASSES)
 
-        nc.vector.tensor_tensor(out=docs_over_sigma[:], in0=inv_sigma[:], in1=docs_sb[last], op=MULT)
-        sum_products(last - 2)
-        divide(last - 1, 0)
-        divide(last - 1, 1)
-        store_concepts(last - 1)
-        score_on_vector(last - 1)
-        concepts_last = work.tile([P, N], F32, name="concepts", tag="concepts", bufs=6)
-        products_last = work.tile([P, N], F32, name="products", tag="products", bufs=3)
-        parts = [slice(0, HALF)] + [slice(c, c + P) for c in range(HALF, N, P)]
+        sum_products(LAST - 2)
+        finish(LAST - 1)
+        sum_products(LAST - 1)
+
+        new_output_tiles(LAST)
         stored = 0
-        for part, cols in enumerate(parts):
-            sums = acc_bank(last, 0)[:] if part == 0 else next_turn_bank()[:, 0, 0, :]
+        for part, cols in enumerate(last_parts):
+            bank = sum_bank(LAST, 0)[:] if part == 0 else next_turn_bank()[:, 0, 0, :]
             for g in range(PASSES):
-                multiply_into(sums, last, g, cols)
-            nc.vector.scalar_tensor_tensor(
-                out=products_last[:, cols],
-                in0=sums,
-                scalar=1.0,
-                in1=docs_over_sigma[:, cols],
-                op0=MULT,
-                op1=MULT,
-                accum_out=last_parts[:, part : part + 1],
+                multiply_into(bank, LAST, g, cols)
+            multiply_and_sum(
+                products[LAST][:, cols], bank, last_docs_over_sigma[:, cols], last_part_scores[:, part : part + 1]
             )
-            nc.vector.tensor_tensor(out=concepts_last[:, cols], in0=sums, in1=inv_sigma[:, cols], op=MULT)
+            divide(LAST, cols, bank)
             if part % 2 == 0:
-                ready = slice(stored, cols.stop)
-                nc.sync.dma_start(out=concepts_v[:, last, ready], in_=concepts_last[:, ready])
+                store_concepts(LAST, slice(stored, cols.stop))
                 stored = cols.stop
-        nc.vector.reduce_sum(out=scores[:, last : last + 1], in_=last_parts[:], axis=mybir.AxisListType.X)
+        nc.vector.reduce_sum(out=scores[:, LAST : LAST + 1], in_=last_part_scores[:], axis=mybir.AxisListType.X)
         nc.scalar.dma_start(out=scores_v, in_=scores[:])

@@ -56,11 +56,11 @@ def tile_lsi_query_fold_in_s1_kernel(
         vec_words = keep.tile([P, PASSES + SIGMA_ROWS, 2], F32)
         inv_sigma_cols = keep.tile([P, SIGMA_ROWS * PACK], F32)
         inv_sigma = keep.tile([P, N], F32)
-        ut_scales = keep.tile([P, TAIL_PASSES, N], U8, align_bytes=64)
-        uh_codes = keep.tile([P, HEAD_PASSES, N], U32, align_bytes=64)
-        uh_scales = keep.tile([P, HEAD_PASSES, N], U8, align_bytes=64)
+        ut_scales = keep.tile([P, TAIL_PASSES, N], U8, align_bytes=256)
+        uh_codes = keep.tile([P, HEAD_PASSES, N], U32, align_bytes=256)
+        uh_scales = keep.tile([P, HEAD_PASSES, N], U8, align_bytes=256)
         scores = keep.tile([P, TILES], F32)
-        last_parts = [slice(0, HALF)] + [slice(c, c + P) for c in range(HALF, N, P)]
+        last_parts = [slice(0, HALF), slice(HALF, N - 2 * P), slice(N - 2 * P, N - P), slice(N - P, N)]
         last_part_scores = keep.tile([P, len(last_parts)], F32)
         last_docs_over_sigma = keep.tile([P, N], F32)
 
@@ -98,7 +98,7 @@ def tile_lsi_query_fold_in_s1_kernel(
                     tf_words[m + i, first + g] = words[:, i, g]
 
         def load_ut_words(pair):
-            ut_words[pair] = keep.tile([P, 2, 2 * N], U8, name="ut_words_%d" % pair, align_bytes=64)
+            ut_words[pair] = keep.tile([P, 2, 2 * N], U8, name="ut_words_%d" % pair, align_bytes=256)
             nc.sync.dma_start(
                 out=ut_words[pair][:].bitcast(I32),
                 in_=u_tail_words[2 * pair : 2 * pair + 2].rearrange("g p n -> p g n").bitcast(I32),
@@ -149,9 +149,9 @@ def tile_lsi_query_fold_in_s1_kernel(
 
         def weigh(m, pair):
             if m not in x_bf16:
-                x_bf16[m] = work.tile([P, PASSES, P, PACK], BF16, name="x_bf16", tag="x_bf16", align_bytes=64)
-                x_codes[m] = work.tile([P, PASSES, P], U32, name="x_codes", tag="x_codes", bufs=3, align_bytes=64)
-                x_scales[m] = work.tile([P, PASSES, P], U8, name="x_scales", tag="x_scales", bufs=3, align_bytes=64)
+                x_bf16[m] = work.tile([P, PASSES, P, PACK], BF16, name="x_bf16", tag="x_bf16", align_bytes=256)
+                x_codes[m] = work.tile([P, PASSES, P], U32, name="x_codes", tag="x_codes", bufs=3, align_bytes=256)
+                x_scales[m] = work.tile([P, PASSES, P], U8, name="x_scales", tag="x_scales", bufs=3, align_bytes=256)
             both_passes = slice(2 * pair, 2 * pair + 2)
             idf = vec_words[:, both_passes, :].bitcast(BF16).rearrange("p g (u e) -> p g u e", e=2)
             nc.vector.tensor_tensor(
@@ -171,7 +171,7 @@ def tile_lsi_query_fold_in_s1_kernel(
 
 
         def interleave_u_head(g, h, copy):
-            uh_bf16[g, h] = work.tile([P, HALF, PACK], BF16, name="uh_bf16", tag="uh_bf16", align_bytes=64)
+            uh_bf16[g, h] = work.tile([P, HALF, PACK], BF16, name="uh_bf16", tag="uh_bf16", align_bytes=256)
             copy(
                 out=uh_bf16[g, h][:].rearrange("p (c i) t -> p c t i", i=4),
                 in_=uh_rows[g][:, :, half_cols(h)].rearrange("p t (c i) -> p c t i", i=4),
@@ -370,14 +370,17 @@ def tile_lsi_query_fold_in_s1_kernel(
         new_output_tiles(LAST)
         stored = 0
         for part, cols in enumerate(last_parts):
-            bank = sum_bank(LAST, 0)[:] if part == 0 else next_turn_bank()[:, 0, 0, :]
-            for g in range(PASSES):
-                multiply_into(bank, LAST, g, cols)
+            width = cols.stop - cols.start
+            bank = next_turn_bank()[:].rearrange("p a b n -> p (a b n)")[:, :width]
+            group = HALF if width == HALF else P
+            for c in range(0, width, group):
+                for g in range(PASSES):
+                    multiply_into(bank[:, c : c + group], LAST, g, slice(cols.start + c, cols.start + c + group))
             multiply_and_sum(
                 products[LAST][:, cols], bank, last_docs_over_sigma[:, cols], last_part_scores[:, part : part + 1]
             )
             divide(LAST, cols, bank)
-            if part % 2 == 0:
+            if part != 2:
                 store_concepts(LAST, slice(stored, cols.stop))
                 stored = cols.stop
         nc.vector.reduce_sum(out=scores[:, LAST : LAST + 1], in_=last_part_scores[:], axis=mybir.AxisListType.X)

from contextlib import ExitStack

import concourse.mybir as mybir
from concourse.masks import make_identity

M, KH, KT, N = 1024, 1024, 3072, 1024
FLOPS = 2 * M * (KH + KT) * N

F32 = mybir.dt.float32
BF16 = mybir.dt.bfloat16
I32 = mybir.dt.int32
U32 = mybir.dt.uint32
U8 = mybir.dt.uint8
FP8X4 = mybir.dt.float8_e4m3fn_x4
FP4X4 = mybir.dt.float4_e2m1fn_x4
MULT = mybir.AluOpType.mult
COPY = mybir.ActivationFunctionType.Copy

P = 128
PACK = 4
K_PASS = P * PACK
WORDS = K_PASS // 2
TAIL_PASSES = KT // K_PASS
HEAD_PASSES = KH // K_PASS
PASSES = TAIL_PASSES + HEAD_PASSES
PAIRS = PASSES // 2
TILES = M // P
LAST = TILES - 1
HALF = 512
SIGMA_ROWS = N // K_PASS
TURN_BANKS = 4
CONCEPT_BUFS = 6
PRODUCT_BUFS = 4
SCORE_FIRST_TILE_IN = 4
SCALE_LAST_DOCS_IN = 5


def tile_lsi_query_fold_in_s1_kernel(
    tc, tf_head, tf_tail, idf_head, idf_tail, u_head, u_tail_words, u_tail_scales, sigma, docs, out_0, out_1
):
    nc = tc.nc
    tf_tail_v = tf_tail.rearrange("(p m) k -> p m k", m=TILES)
    tf_head_v = tf_head.rearrange("(p m) k -> p m k", m=TILES)
    docs_v = docs.rearrange("(p m) n -> p m n", m=TILES)
    concepts_v = out_0.rearrange("(p m) n -> p m n", m=TILES)
    scores_v = out_1.rearrange("(p m) o -> p (m o)", m=TILES)

    with ExitStack() as ctx:
        keep = ctx.enter_context(tc.tile_pool(name="keep", bufs=1))
        work = ctx.enter_context(tc.tile_pool(name="work", bufs=2))
        psum = ctx.enter_context(tc.psum_pool(name="psum", bufs=1))
        ctx.enter_context(tc.manual_schedule())

        ident = keep.tile([P, P], F32)
        vec_rows = keep.tile([P, K_PASS], BF16)
        vec_words = keep.tile([P, PASSES + SIGMA_ROWS, 2], F32)
        inv_sigma_cols = keep.tile([P, SIGMA_ROWS * PACK], F32)
        inv_sigma = keep.tile([P, N], F32)
        ut_scales = keep.tile([P, TAIL_PASSES, N], U8, align_bytes=256)
        uh_codes = keep.tile([P, HEAD_PASSES, N], U32, align_bytes=256)
        uh_scales = keep.tile([P, HEAD_PASSES, N], U8, align_bytes=256)
        scores = keep.tile([P, TILES], F32)
        last_parts = [slice(0, HALF), slice(HALF, N - 2 * P), slice(N - 2 * P, N - P), slice(N - P, N)]
        last_part_scores = keep.tile([P, len(last_parts)], F32)
        last_docs_over_sigma = keep.tile([P, N], F32)

        tf_runs = {}
        tf_words = {}
        sorted_words = {}
        turned = {}
        x_bf16 = {}
        x_codes = {}
        x_scales = {}
        ut_words = {}
        uh_rows = {}
        uh_bf16 = {}
        docs_sb = {}
        sums = {}
        concepts = {}
        products = {}
        turn_banks_taken = []

        def half_cols(h):
            return slice(h * HALF, (h + 1) * HALF)


        def load_tf(m, tiles, first, count):
            source, start = (tf_tail_v, first) if first < TAIL_PASSES else (tf_head_v, first - TAIL_PASSES)
            raw = keep.tile([P, tiles * count * K_PASS], BF16, name="tf_%d_%d" % (m, first))
            nc.sync.dma_start(
                out=raw[:].rearrange("p (m k) -> p m k", m=tiles),
                in_=source[:, m : m + tiles, start * K_PASS : (start + count) * K_PASS],
            )
            words = raw[:].bitcast(F32).rearrange("p (m g w) -> p m g w", m=tiles, w=WORDS)
            for i in range(tiles):
                tf_runs[m + i, first] = words[:, i]
                for g in range(count):
                    tf_words[m + i, first + g] = words[:, i, g]

        def load_ut_words(pair):
            ut_words[pair] = keep.tile([P, 2, 2 * N], U8, name="ut_words_%d" % pair, align_bytes=256)
            nc.sync.dma_start(
                out=ut_words[pair][:].bitcast(I32),
                in_=u_tail_words[2 * pair : 2 * pair + 2].rearrange("g p n -> p g n").bitcast(I32),
            )

        def load_ut_scales():
            by_row = u_tail_scales.rearrange("g (q r) n -> r q g n", r=4)
            for r in range(4):
                nc.sync.dma_start(out=ut_scales[r:P:32].bitcast(I32), in_=by_row[r].bitcast(I32))

        def load_u_head(g):
            uh_rows[g] = keep.tile([P, PACK, N], BF16, name="u_head_%d" % g)
            nc.sync.dma_start(
                out=uh_rows[g][:],
                in_=u_head[g * K_PASS : (g + 1) * K_PASS, :].rearrange("(p t) n -> p t n", t=PACK),
            )

        def load_docs(m):
            raw = keep.tile([P, 2, N], BF16, name="docs_%d" % m)
            nc.sync.dma_start(out=raw[:], in_=docs_v[:, m : m + 2, :])
            docs_sb[m] = raw[:, 0, :]
            docs_sb[m + 1] = raw[:, 1, :]


        def next_turn_bank():
            tag = "turn%d" % (len(turn_banks_taken) % TURN_BANKS)
            turn_banks_taken.append(tag)
            return psum.tile([P, 2, 2, P], F32, name=tag, tag=tag)

        def sort_words(m, first, out):
            run = tf_runs[m, first]
            nc.scalar.copy(out=out, in_=run.rearrange("p g (w u) -> p g u w", u=2))
            for g in range(run.shape[1]):
                sorted_words[m, first + g] = out[:, g]

        def sort_tile(m):
            out = work.tile([P, PASSES, 2, P], F32, name="sorted", tag="sorted")
            sort_words(m, 0, out[:, :TAIL_PASSES])
            sort_words(m, TAIL_PASSES, out[:, TAIL_PASSES:])

        def turn(m, pair):
            turned[m, pair] = next_turn_bank()
            for i in range(2):
                g = 2 * pair + i
                for u in range(2):
                    words = sorted_words[m, g][:, u, :] if (m, g) in sorted_words else tf_words[m, g][:, u:WORDS:2]
                    nc.tensor.transpose(turned[m, pair][:, u, i, :], words, ident[:])

        def weigh(m, pair):
            if m not in x_bf16:
                x_bf16[m] = work.tile([P, PASSES, P, PACK], BF16, name="x_bf16", tag="x_bf16", align_bytes=256)
                x_codes[m] = work.tile([P, PASSES, P], U32, name="x_codes", tag="x_codes", bufs=3, align_bytes=256)
                x_scales[m] = work.tile([P, PASSES, P], U8, name="x_scales", tag="x_scales", bufs=3, align_bytes=256)
            both_passes = slice(2 * pair, 2 * pair + 2)
            idf = vec_words[:, both_passes, :].bitcast(BF16).rearrange("p g (u e) -> p g u e", e=2)
            nc.vector.tensor_tensor(
                out=x_bf16[m][:, both_passes].rearrange("p g r (u e) -> p g r u e", e=2),
                in0=turned[m, pair][:].bitcast(BF16).rearrange("p u g (r e) -> p g r u e", e=2),
                in1=idf.unsqueeze(2).broadcast_to([P, 2, P, 2, 2]),
                op=MULT,
            )

        def quantize_x(m, first, count):
            passes = slice(first, first + count)
            nc.vector.quantize_mx(
                out=x_codes[m][:, passes].rearrange("p g r -> p (g r)").bitcast(FP8X4),
                scales=x_scales[m][:, passes].rearrange("p g r -> p (g r)"),
                in_=x_bf16[m][:, passes].rearrange("p g r t -> p (g r t)"),
            )


        def interleave_u_head(g, h, copy):
            uh_bf16[g, h] = work.tile([P, HALF, PACK], BF16, name="uh_bf16", tag="uh_bf16", align_bytes=256)
            copy(
                out=uh_bf16[g, h][:].rearrange("p (c i) t -> p c t i", i=4),
                in_=uh_rows[g][:, :, half_cols(h)].rearrange("p t (c i) -> p c t i", i=4),
            )

        def quantize_u_head(g, h):
            nc.vector.quantize_mx(
                out=uh_codes[:, g, half_cols(h)].bitcast(FP8X4),
                scales=uh_scales[:, g, half_cols(h)],
                in_=uh_bf16[g, h][:].rearrange("p n t -> p (n t)"),
            )


        def multiply_into(out, m, g, cols):
            if g < TAIL_PASSES:
                rhs = ut_words[g // 2][:, g % 2, 2 * cols.start : 2 * cols.stop].bitcast(FP4X4)
                rhs_scale = ut_scales[:, g, cols]
            else:
                rhs = uh_codes[:, g - TAIL_PASSES, cols].bitcast(FP8X4)
                rhs_scale = uh_scales[:, g - TAIL_PASSES, cols]
            nc.tensor.matmul_mx(
                out=out,
                lhsT=x_codes[m][:, g, :].bitcast(FP8X4),
                lhsT_scale=x_scales[m][:, g, :],
                rhs=rhs,
                rhs_scale=rhs_scale,
                start=(g == 0),
                stop=(g == PASSES - 1),
            )

        def sum_bank(m, h):
            if (m, h) not in sums:
                tag = "sums%d" % (2 * (m % 2) + h)
                sums[m, h] = psum.tile([P, HALF], F32, name=tag, tag=tag)
            return sums[m, h]

        def multiply(m, g, h):
            multiply_into(sum_bank(m, h)[:], m, g, half_cols(h))

        def multiply_passes(m, first, stop):
            for g in range(first, stop):
                for h in range(2):
                    multiply(m, g, h)


        def new_output_tiles(m):
            concepts[m] = work.tile([P, N], F32, name="concepts", tag="concepts", bufs=CONCEPT_BUFS)
            products[m] = work.tile([P, N], F32, name="products", tag="products", bufs=PRODUCT_BUFS)

        def divide(m, cols, bank):
            nc.vector.tensor_tensor(out=concepts[m][:, cols], in0=bank, in1=inv_sigma[:, cols], op=MULT)

        def store_concepts(m, cols):
            nc.sync.dma_start(out=concepts_v[:, m, cols], in_=concepts[m][:, cols])

        def finish(m):
            new_output_tiles(m)
            for h in range(2):
                cols = half_cols(h)
                divide(m, cols, sums[m, h][:])
                nc.gpsimd.tensor_tensor(
                    out=products[m][:, cols], in0=concepts[m][:, cols], in1=docs_sb[m][:, cols], op=MULT
                )
            store_concepts(m, slice(0, N))

        def sum_products(m):
            nc.scalar.activation(out=products[m][:], in_=products[m][:], func=COPY, accum_out=scores[:, m : m + 1])

        def multiply_and_sum(out, in0, in1, total):
            nc.vector.scalar_tensor_tensor(out=out, in0=in0, scalar=1.0, in1=in1, op0=MULT, op1=MULT, accum_out=total)

        def spread_inv_sigma(h):
            spread = next_turn_bank()[:].rearrange("p a b n -> p (a b) n")
            for t in range(PACK):
                column = inv_sigma_cols[:, PACK * h + t : PACK * h + t + 1]
                nc.tensor.transpose(spread[:, t, :], column.to_broadcast([P, P]), ident[:])
            nc.scalar.copy(
                out=inv_sigma[:, half_cols(h)].rearrange("p (n t) -> p n t", t=PACK),
                in_=spread.rearrange("p t n -> p n t"),
            )

        def first_two(step, *args):
            step(0, *args)
            step(1, *args)

        nc.vector.memset(vec_rows[:].bitcast(F32), 0.0)
        make_identity(nc, ident[:])
        nc.vector.memset(ut_scales[:].bitcast(I32), 0)

        load_tf(0, 2, 0, 2)
        nc.scalar.dma_start(out=vec_rows[:TAIL_PASSES], in_=idf_tail.rearrange("(g k) -> g k", k=K_PASS))
        nc.scalar.dma_start(out=vec_rows[TAIL_PASSES:PASSES], in_=idf_head.rearrange("(g k) -> g k", k=K_PASS))
        nc.scalar.dma_start(
            out=vec_rows[PASSES : PASSES + SIGMA_ROWS], in_=sigma.rearrange("(h k) -> h k", k=K_PASS)
        )
        load_ut_words(0)
        load_tf(0, 2, 2, 2)
        load_ut_scales()
        load_tf(0, 2, 4, 2)
        load_ut_words(1)
        load_u_head(0)
        load_tf(0, 2, TAIL_PASSES, HEAD_PASSES)
        load_ut_words(2)
        load_u_head(1)
        for m in range(2, TILES, 2):
            load_tf(m, 1, 0, TAIL_PASSES)
            load_tf(m, 2, TAIL_PASSES, HEAD_PASSES)
            load_tf(m + 1, 1, 0, TAIL_PASSES)
            load_docs(m - 2)
        load_docs(TILES - 2)

        vec_bank = next_turn_bank()
        for u in range(2):
            nc.tensor.transpose(vec_bank[:, u, 0, :], vec_rows[:].bitcast(F32)[:, u:WORDS:2], ident[:])
        nc.vector.tensor_copy(
            out=vec_words[:], in_=vec_bank[:, :, 0, : PASSES + SIGMA_ROWS].rearrange("p u g -> p g u")
        )
        nc.vector.reciprocal(
            out=inv_sigma_cols[:], in_=vec_words[:, PASSES:, :].bitcast(BF16).rearrange("p h t -> p (h t)")
        )

        first_two(turn, 0)
        first_two(weigh, 0)
        first_two(quantize_x, 0, 2)
        spread_inv_sigma(0)
        first_two(turn, 1)
        spread_inv_sigma(1)
        first_two(weigh, 1)
        first_two(quantize_x, 2, 2)
        sorted_pair = work.tile([P, 2, 2, 2, P], F32, name="sorted", tag="sorted")
        for m in range(2):
            sort_words(m, 4, sorted_pair[:, m])
        first_two(multiply_passes, 0, 2)
        first_two(turn, 2)
        first_two(weigh, 2)
        first_two(quantize_x, 4, 2)
        first_two(multiply_passes, 2, 4)
        interleave_u_head(0, 0, nc.scalar.copy)
        interleave_u_head(0, 1, nc.vector.tensor_copy)
        first_two(turn, 3)
        weigh(0, 3)
        quantize_u_head(0, 1)
        weigh(1, 3)
        quantize_u_head(0, 0)
        first_two(quantize_x, 6, 2)
        first_two(multiply_passes, 4, 6)
        first_two(multiply_passes, 6, 7)

        interleave_u_head(1, 0, nc.scalar.copy)
        interleave_u_head(1, 1, nc.vector.tensor_copy)
        turn(2, 0)
        turn(2, 1)
        quantize_u_head(1, 1)
        quantize_u_head(1, 0)
        weigh(2, 0)
        weigh(2, 1)
        first_two(multiply, PASSES - 1, 1)
        first_two(multiply, PASSES - 1, 0)
        turn(2, 2)
        turn(2, 3)
        sort_tile(3)
        new_output_tiles(0)
        divide(0, half_cols(1), sums[0, 1][:])
        quantize_x(2, 0, PASSES // 2)
        divide(0, half_cols(0), sums[0, 0][:])
        store_concepts(0, slice(0, N))
        weigh(2, 2)
        weigh(2, 3)
        for h in (1, 0):
            for g in range(PASSES // 2):
                multiply(2, g, h)
        quantize_x(2, PASSES // 2, PASSES // 2)

        for m in range(2, LAST):
            for pair in range(PAIRS):
                turn(m + 1, pair)
            if m + 2 < TILES:
                sort_tile(m + 2)
            if m > 2:
                sum_products(m - 2)
            finish(m - 1)
            for pair in range(PAIRS):
                weigh(m + 1, pair)
            quantize_x(m + 1, 0, PASSES // 2)
            quantize_x(m + 1, PASSES // 2, PASSES // 2)
            if m == SCORE_FIRST_TILE_IN:
                multiply_and_sum(products[0][:], concepts[0][:], docs_sb[0], scores[:, 0:1])
            if m == SCALE_LAST_DOCS_IN:
                nc.vector.tensor_tensor(out=last_docs_over_sigma[:], in0=inv_sigma[:], in1=docs_sb[LAST], op=MULT)
            multiply_passes(m, PASSES // 2 if m == 2 else 0, PASSES)

        sum_products(LAST - 2)
        finish(LAST - 1)
        sum_products(LAST - 1)

        new_output_tiles(LAST)
        stored = 0
        for part, cols in enumerate(last_parts):
            width = cols.stop - cols.start
            bank = next_turn_bank()[:].rearrange("p a b n -> p (a b n)")[:, :width]
            group = HALF if width == HALF else P
            for c in range(0, width, group):
                for g in range(PASSES):
                    multiply_into(bank[:, c : c + group], LAST, g, slice(cols.start + c, cols.start + c + group))
            multiply_and_sum(
                products[LAST][:, cols], bank, last_docs_over_sigma[:, cols], last_part_scores[:, part : part + 1]
            )
            divide(LAST, cols, bank)
            if part != 2:
                store_concepts(LAST, slice(stored, cols.stop))
                stored = cols.stop
        nc.vector.reduce_sum(out=scores[:, LAST : LAST + 1], in_=last_part_scores[:], axis=mybir.AxisListType.X)
        nc.scalar.dma_start(out=scores_v, in_=scores[:])
